import numpy as np
import ml_dtypes

BF16 = ml_dtypes.bfloat16


def bf(x):
    return np.asarray(x, np.float32).astype(BF16)


def f32(x):
    return np.asarray(x, np.float32)


def f64(x):
    return np.asarray(x).astype(np.float64)


def striped(idx):
    return np.tile(idx.reshape(-1, 16).T, (8, 1))


S, K, M, N, V, D = 512, 512, 128, 512, 256, 2


def setup_inputs():
    return {"table": bf(np.random.standard_normal((K, S))), "w": bf(np.random.standard_normal((D, K, M)) / np.sqrt(K)), "s": f32(0.5 + np.random.random_sample((M, 1))), "offs": striped(np.random.permutation(np.tile(np.arange(S), 2))[:N])}


def reference(table, w, s, offs):
    idx = offs[:16].T.reshape(-1)
    x = f64(table)[:, idx]
    p = f64(w)[0].T @ x[:, :V]
    q = f64(w)[1].T @ x[:, V:]
    return p * q * f64(s)

@@ -1,0 +1,46 @@
+import concourse.mybir as mybir
+
+BF16, F32, U16 = mybir.dt.bfloat16, mybir.dt.float32, mybir.dt.uint16
+MULT = mybir.AluOpType.mult
+
+P = 128
+GROUP = 16
+K, M, V = 512, 128, 256
+FLOPS = 2 * 2 * K * M * V + 2 * M * V
+
+
+def tile_rows_pair_mul_rep_kernel(tc, table, w, s, offs, out):
+    nc = tc.nc
+    nodes = table.shape[1]
+    blocks = K // P
+    cols = V // GROUP
+    with (
+        tc.tile_pool(name="held", bufs=1) as held,
+        tc.psum_pool(name="psum", bufs=1) as psum,
+    ):
+        offsets = held.tile([P, 2 * cols], U16, name="offsets")
+        nc.sync.dma_start(offsets[:], offs)
+        weights = held.tile([P, 2, blocks, M], BF16, name="weights")
+        nc.scalar.dma_start(weights[:], w.rearrange("d (b p) m -> p d b m", p=P))
+        gain = held.tile([P, 1], F32, name="gain")
+        nc.scalar.dma_start(gain[:], s)
+        windows = [held.tile([P, nodes], BF16, name=f"window{b}") for b in range(blocks)]
+        for b in range(blocks):
+            nc.sync.dma_start(windows[b][:], table[b * P:(b + 1) * P, :])
+
+        sums = [psum.tile([P, V], F32, name=f"sum{half}") for half in range(2)]
+        for half in range(2):
+            for b in range(blocks):
+                nc.tensor.matmul(
+                    sums[half][:],
+                    weights[:, half, b, :],
+                    windows[b][:].indirect(offsets[:, half * cols:(half + 1) * cols]),
+                    start=(b == 0),
+                    stop=(b == blocks - 1),
+                )
+
+        first = held.tile([P, V], F32, name="first")
+        nc.vector.tensor_scalar(first[:], sums[0][:], gain[:], None, MULT)
+        result = held.tile([P, V], F32, name="result")
+        nc.vector.tensor_tensor(result[:], sums[1][:], first[:], MULT)
+        nc.sync.dma_start(out, result[:])

@@ -12,32 +12,35 @@ FLOPS = 2 * 2 * K * M * V + 2 * M * V
 def tile_rows_pair_mul_rep_kernel(tc, table, w, s, offs, out):
     nc = tc.nc
     nodes = table.shape[1]
-    blocks = K // P
     cols = V // GROUP
+    table_rows = table.rearrange("(p stage j) n -> p stage j n", stage=2, j=2)
+    weight_rows = w.rearrange("d (p stage j) m -> p stage d j m", stage=2, j=2)
     with (
         tc.tile_pool(name="held", bufs=1) as held,
         tc.psum_pool(name="psum", bufs=1) as psum,
     ):
         offsets = held.tile([P, 2 * cols], U16, name="offsets")
-        nc.sync.dma_start(offsets[:], offs)
-        weights = held.tile([P, 2, blocks, M], BF16, name="weights")
-        nc.scalar.dma_start(weights[:], w.rearrange("d (b p) m -> p d b m", p=P))
+        windows = [held.tile([P, 2, nodes], BF16, name=f"windows{stage}") for stage in range(2)]
+        weights = [held.tile([P, 2, 2, M], BF16, name=f"weights{stage}") for stage in range(2)]
         gain = held.tile([P, 1], F32, name="gain")
+        nc.sync.dma_start(windows[0][:], table_rows[:, 0])
+        nc.scalar.dma_start(weights[0][:], weight_rows[:, 0])
+        nc.sync.dma_start(offsets[:], offs)
+        nc.sync.dma_start(windows[1][:], table_rows[:, 1])
+        nc.scalar.dma_start(weights[1][:], weight_rows[:, 1])
         nc.scalar.dma_start(gain[:], s)
-        windows = [held.tile([P, nodes], BF16, name=f"window{b}") for b in range(blocks)]
-        for b in range(blocks):
-            nc.sync.dma_start(windows[b][:], table[b * P:(b + 1) * P, :])
 
-        sums = [psum.tile([P, V], F32, name=f"sum{half}") for half in range(2)]
-        for half in range(2):
-            for b in range(blocks):
-                nc.tensor.matmul(
-                    sums[half][:],
-                    weights[:, half, b, :],
-                    windows[b][:].indirect(offsets[:, half * cols:(half + 1) * cols]),
-                    start=(b == 0),
-                    stop=(b == blocks - 1),
-                )
+        sums = [psum.tile([P, V], F32, name=f"sum{end}") for end in range(2)]
+        for stage in range(2):
+            for end in range(2):
+                for j in range(2):
+                    nc.tensor.matmul(
+                        sums[end][:],
+                        weights[stage][:, end, j, :],
+                        windows[stage][:, j, :].indirect(offsets[:, end * cols:(end + 1) * cols]),
+                        start=(stage == 0 and j == 0),
+                        stop=(stage == 1 and j == 1),
+                    )
 
         first = held.tile([P, V], F32, name="first")
         nc.vector.tensor_scalar(first[:], sums[0][:], gain[:], None, MULT)

import concourse.mybir as mybir

BF16, F32, U16 = mybir.dt.bfloat16, mybir.dt.float32, mybir.dt.uint16
MULT = mybir.AluOpType.mult

P = 128
GROUP = 16
K, M, V = 512, 128, 256
FLOPS = 2 * 2 * K * M * V + 2 * M * V


def tile_rows_pair_mul_rep_kernel(tc, table, w, s, offs, out):
    nc = tc.nc
    nodes = table.shape[1]
    cols = V // GROUP
    table_rows = table.rearrange("(p stage j) n -> p stage j n", stage=2, j=2)
    weight_rows = w.rearrange("d (p stage j) m -> p stage d j m", stage=2, j=2)
    with (
        tc.tile_pool(name="held", bufs=1) as held,
        tc.psum_pool(name="psum", bufs=1) as psum,
    ):
        offsets = held.tile([P, 2 * cols], U16, name="offsets")
        windows = [held.tile([P, 2, nodes], BF16, name=f"windows{stage}") for stage in range(2)]
        weights = [held.tile([P, 2, 2, M], BF16, name=f"weights{stage}") for stage in range(2)]
        gain = held.tile([P, 1], F32, name="gain")
        nc.sync.dma_start(windows[0][:], table_rows[:, 0])
        nc.scalar.dma_start(weights[0][:], weight_rows[:, 0])
        nc.sync.dma_start(offsets[:], offs)
        nc.sync.dma_start(windows[1][:], table_rows[:, 1])
        nc.scalar.dma_start(weights[1][:], weight_rows[:, 1])
        nc.scalar.dma_start(gain[:], s)

        sums = [psum.tile([P, V], F32, name=f"sum{end}") for end in range(2)]
        for stage in range(2):
            for end in range(2):
                for j in range(2):
                    nc.tensor.matmul(
                        sums[end][:],
                        weights[stage][:, end, j, :],
                        windows[stage][:, j, :].indirect(offsets[:, end * cols:(end + 1) * cols]),
                        start=(stage == 0 and j == 0),
                        stop=(stage == 1 and j == 1),
                    )

        first = held.tile([P, V], F32, name="first")
        nc.vector.tensor_scalar(first[:], sums[0][:], gain[:], None, MULT)
        result = held.tile([P, V], F32, name="result")
        nc.vector.tensor_tensor(result[:], sums[1][:], first[:], MULT)
        nc.sync.dma_start(out, result[:])
